import numpy as np
import ml_dtypes


def mxq(x, axis, fmt="e4m3"):
    dtype, down = {"e4m3": (ml_dtypes.float8_e4m3fn, 7), "e5m2": (ml_dtypes.float8_e5m2, 14)}[fmt]
    v = np.moveaxis(np.asarray(x, np.float32).astype(ml_dtypes.bfloat16).astype(np.float64), axis, -1)
    blocks = v.reshape(v.shape[:-1] + (-1, 32))
    amax = np.abs(blocks).max(-1, keepdims=True)
    byte = np.maximum(np.where(amax > 0, np.frexp(amax)[1] - 1 + 127, 0) - down, 1)
    scale = np.exp2(byte - 127.0)
    codes = (blocks / scale).astype(np.float32).astype(dtype).astype(np.float64)
    return np.moveaxis((codes * scale).reshape(v.shape), -1, axis)


WIDE = False


def mx_kscale(k):
    if not WIDE:
        return np.ones(k)
    levels = np.array([10, -10, 5, -5, 0])
    if k % 512:
        return np.exp2(np.random.permutation(np.resize(levels, k // 32))).repeat(32)
    a = np.empty((k // 512, 16))
    for p in range(k // 512):
        a[p, :8] = np.random.permutation(np.resize(levels, 8))
        for g in range(8):
            far = levels[np.abs(levels - a[p, g]) >= 10]
            a[p, g + 8] = far[np.random.randint(len(far))]
    return np.exp2(a.ravel()).repeat(32)


def f64(x):
    return np.asarray(x).astype(np.float64)


def striped(idx):
    return np.tile(idx.reshape(-1, 16).T, (8, 1)).astype(np.uint16)


def unstriped(offs):
    return offs[:16].T.reshape(-1).astype(np.int64)


E2M1 = np.array([0.0, 0.5, 1.0, 1.5, 2.0, 3.0, 4.0, 6.0, -0.0, -0.5, -1.0, -1.5, -2.0, -3.0, -4.0, -6.0])


def pack_weight(w, fmt):
    k, n = w.shape
    w = f64(np.asarray(w, np.float32).astype(ml_dtypes.bfloat16)).reshape(k // 32, 32, n)
    amax = np.abs(w).max(1)
    if fmt == "e4m3":
        byte = np.frexp(amax)[1] - 1 + 127 - 7
    else:
        mant, ex = np.frexp(amax / 6.0)
        byte = np.where(mant > 0.5, ex, ex - 1) + 127
    byte = np.clip(np.where(amax > 0, byte, 1), 1, 254)
    scaled = (w * np.exp2(127.0 - byte)[:, None, :]).reshape(k, n).astype(np.float32)
    by_word = np.ascontiguousarray(scaled.reshape(k // 512, 128, 4, n).transpose(0, 1, 3, 2))
    if fmt == "e4m3":
        words = by_word.astype(ml_dtypes.float8_e4m3fn).view(np.uint8)
    else:
        c = by_word.astype(ml_dtypes.float4_e2m1fn).view(np.uint8) & 0xF
        words = (c[..., 0::2] | (c[..., 1::2] << 4)).reshape(k // 512, 128, 2 * n)
    return np.ascontiguousarray(words), np.ascontiguousarray(byte.astype(np.uint8).reshape(k // 512, 16, n))


def unpack_weight(words, scales, fmt):
    g, _, n = scales.shape
    words = np.ascontiguousarray(words).reshape(g, 128, n, -1)
    if fmt == "e4m3":
        vals = words.view(ml_dtypes.float8_e4m3fn).astype(np.float64)
    else:
        nib = np.empty((g, 128, n, 4), np.uint8)
        nib[..., 0::2] = words & 0xF
        nib[..., 1::2] = words >> 4
        vals = E2M1[nib]
    vals = vals * np.repeat(np.exp2(scales.astype(np.float64) - 127.0), 8, axis=1)[..., None]
    return vals.transpose(0, 1, 3, 2).reshape(g * 512, n)


def gelu(v):
    return 0.5 * v * (1.0 + np.tanh(np.sqrt(2.0 / np.pi) * (v + 0.044715 * v**3)))


K, T, S, H, P, N, P2 = 1024, 4096, 1024, 512, 512, 768, 256

def setup_inputs():
    n = np.random.standard_normal
    s = mx_kscale(K)[:, None]
    u = mx_kscale(H)[:, None]
    tab_words, tab_scales = pack_weight(n((K, T)) * s, "e4m3")
    w1_words, w1_scales = pack_weight(1.2 * n((K, H)) / np.sqrt(K) / s, "e2m1")
    w3_words, w3_scales = pack_weight(0.3 * n((K, H)) / np.sqrt(K) / s, "e4m3")
    return {
        "tab_words": tab_words, "tab_scales": tab_scales,
        "offs": striped(np.random.permutation(T)[:S]),
        "pos1": striped(np.random.permutation(S)[:P]),
        "pos2": striped(np.random.permutation(S)[:P]),
        "pos3": striped(np.random.permutation(P)[:P2]),
        "pos4": striped(np.random.permutation(P)[:P2]),
        "w1_words": w1_words, "w1_scales": w1_scales,
        "w2": (0.52 * n((K, H)) / np.sqrt(K) / s).astype(np.float32),
        "w3_words": w3_words, "w3_scales": w3_scales,
        "gain": (np.exp(0.3 * n(H)) * u[:, 0]).astype(np.float32),
        "w4": (2.0 * n((H, N)) / np.sqrt(H) / u).astype(np.float32),
    }

def reference(tab_words, tab_scales, offs, pos1, pos2, pos3, pos4,
              w1_words, w1_scales, w2, w3_words, w3_scales, gain, w4):
    v = unpack_weight(tab_words, tab_scales, "e4m3")[:, unstriped(offs)]
    w1 = unpack_weight(w1_words, w1_scales, "e2m1")
    w3 = unpack_weight(w3_words, w3_scales, "e4m3")
    r1 = w1.T @ v
    r2 = mxq(f64(w2), 0, "e4m3").T @ v
    r3 = w3.T @ v
    h = (np.tanh(r1) * np.sin(r2) + r3) * f64(gain)[:, None]
    z = np.maximum(h[:, unstriped(pos1)], h[:, unstriped(pos2)])
    y = mxq(f64(w4), 0, "e4m3").T @ mxq(z, 0, "e4m3")
    return y[:, unstriped(pos3)] - y[:, unstriped(pos4)]

@@ -1,0 +1,232 @@
+from contextlib import ExitStack
+
+import concourse.mybir as mybir
+
+K, T, S, H, PAIRS, N, LOTS = 1024, 4096, 1024, 512, 512, 768, 256
+FLOPS = 2 * (3 * K * H * S + H * N * PAIRS)
+
+F32 = mybir.dt.float32
+BF16 = mybir.dt.bfloat16
+I32 = mybir.dt.int32
+U32 = mybir.dt.uint32
+U16 = mybir.dt.uint16
+U8 = mybir.dt.uint8
+FP8X4 = mybir.dt.float8_e4m3fn_x4
+FP4X4 = mybir.dt.float4_e2m1fn_x4
+ACT = mybir.ActivationFunctionType
+ALU = mybir.AluOpType
+
+P = 128
+PACK = 4
+PASSES = K // (P * PACK)
+BANK = 512
+HALVES = S // BANK
+QUADS = 4
+ROWS = 4
+STRIPE = 16
+
+
+def tile_list_seed_tray_contrast_kernel(
+    tc, tab_words, tab_scales, offs, pos1, pos2, pos3, pos4,
+    w1_words, w1_scales, w2, w3_words, w3_scales, gain, w4, out,
+):
+    nc = tc.nc
+    with ExitStack() as ctx:
+        keep = ctx.enter_context(tc.tile_pool(name="keep", bufs=1))
+        ring = ctx.enter_context(tc.tile_pool(name="ring", bufs=4))
+        psum = ctx.enter_context(tc.psum_pool(name="psum", bufs=1))
+
+        def held(shape, dtype, name):
+            return keep.tile(shape, dtype, name=name, align_bytes=64)
+
+        tab_sc = held([P, T], U8, "tab_sc")
+        nc.vector.memset(tab_sc[:].bitcast(I32), 0)
+        w1_sc_raw = held([P, PASSES, H], U8, "w1_sc_raw")
+        nc.gpsimd.memset(w1_sc_raw[:].bitcast(I32), 0)
+        w3_sc_raw = held([P, H], U8, "w3_sc_raw")
+        nc.gpsimd.memset(w3_sc_raw[:].bitcast(I32), 0)
+        v_sc1 = held([P, S], U8, "v_sc1")
+        nc.gpsimd.memset(v_sc1[:].bitcast(I32), 0)
+
+        lists = {}
+
+        def load_list(name, src):
+            lists[name] = keep.tile(list(src.shape), U16, name=name)
+            nc.sync.dma_start(lists[name][:], src)
+
+        def load_packed_scales(plane, scales):
+            for q in range(QUADS):
+                nc.sync.dma_start(
+                    plane[32 * q : 32 * q + PASSES * ROWS, :].bitcast(I32),
+                    scales[:, ROWS * q : ROWS * (q + 1), :].bitcast(I32),
+                )
+
+        def load_table(a):
+            words = held([P, T], I32, "tab%d" % a)
+            nc.sync.dma_start(words[:], tab_words[a].rearrange("p t i -> p (t i)").bitcast(I32))
+            return words
+
+        w1_raw = held([P, PASSES, 2 * H], U8, "w1_raw")
+        nc.sync.dma_start(w1_raw[:].bitcast(I32), w1_words.rearrange("a p c -> p a c").bitcast(I32))
+        load_list("offs", offs)
+        load_list("pos1", pos1)
+        load_packed_scales(tab_sc, tab_scales)
+        tab = [load_table(0)]
+        for q in range(QUADS):
+            nc.sync.dma_start(
+                w1_sc_raw[32 * q : 32 * q + ROWS, :, :].bitcast(I32),
+                w1_scales[:, ROWS * q : ROWS * (q + 1), :].rearrange("a r c -> r a c").bitcast(I32),
+            )
+        load_list("pos2", pos2)
+        tab.append(load_table(1))
+        load_packed_scales(w3_sc_raw, w3_scales)
+        w2_pieces = ((0, 0, H), (1, 0, H // 2), (1, H // 2, H))
+        w2_raw = []
+        for a, c0, c1 in w2_pieces:
+            w2_raw.append(held([P, PACK, c1 - c0], F32, "w2_raw%d_%d" % (a, c0)))
+            rows = w2[a * P * PACK : (a + 1) * P * PACK, c0:c1]
+            nc.sync.dma_start(w2_raw[-1][:], rows.rearrange("(p j) c -> p j c", j=PACK))
+        w3_raw = held([P, PASSES, H], I32, "w3_raw")
+        nc.sync.dma_start(w3_raw[:], w3_words.rearrange("a p c i -> p a (c i)").bitcast(I32))
+        gain_sb = held([P, PACK], F32, "gain_sb")
+        nc.sync.dma_start(gain_sb[:], gain.rearrange("(p t) -> p t", t=PACK))
+        w4_raw = held([P, PACK, N], F32, "w4_raw")
+        nc.sync.dma_start(w4_raw[:], w4.rearrange("(p j) n -> p j n", j=PACK))
+        load_list("pos3", pos3)
+        load_list("pos4", pos4)
+
+        v_sc0 = held([P, S], U8, "v_sc0")
+        nc.vector.tensor_copy(v_sc0[:], tab_sc[:].indirect(lists["offs"][:]))
+        live = 32 * (QUADS - 1) + ROWS
+        nc.scalar.dma_start(v_sc1[0:live, :].bitcast(I32), v_sc0[ROWS : ROWS + live, :].bitcast(I32))
+        v_sc = (v_sc0, v_sc1)
+        w1_codes = held([P, PASSES, 2 * H], U8, "w1_codes")
+        nc.vector.tensor_copy(
+            w1_codes[:].rearrange("p a (t m b) -> p a t m b", t=PACK, b=2),
+            w1_raw[:].rearrange("p a (m t b) -> p a t m b", t=PACK, b=2),
+        )
+        v = {}
+        cols = BANK // STRIPE
+        for a in range(PASSES):
+            for half in range(HALVES):
+                v[a, half] = held([P, BANK], U32, "v%d_%d" % (a, half))
+                picks = lists["offs"][:, half * cols : (half + 1) * cols]
+                nc.vector.tensor_copy(v[a, half][:], tab[a][:].bitcast(U32).indirect(picks))
+        w1_sc = held([P, PASSES, H], U8, "w1_sc")
+        nc.vector.tensor_copy(
+            w1_sc[:].rearrange("p a (t m) -> p a t m", t=PACK),
+            w1_sc_raw[:].rearrange("p a (m t) -> p a t m", t=PACK),
+        )
+        w3_sc = held([P, H], U8, "w3_sc")
+        nc.vector.tensor_copy(
+            w3_sc[:].rearrange("p (t m) -> p t m", t=PACK),
+            w3_sc_raw[:].rearrange("p (m t) -> p t m", t=PACK),
+        )
+
+        def product(tag, bufs, weights, t, half):
+            acc = psum.tile([P, BANK], F32, name=tag, tag=tag, bufs=bufs)
+            for a in range(PASSES):
+                codes, scales = weights(a, t)
+                nc.tensor.matmul_mx(
+                    acc[:], codes, scales,
+                    v[a, half][:].bitcast(FP8X4), v_sc[a][:, half * BANK : (half + 1) * BANK],
+                    start=(a == 0), stop=(a == PASSES - 1),
+                )
+            return acc
+
+        def w1_slice(a, t):
+            return w1_codes[:, a, 2 * P * t : 2 * P * (t + 1)].bitcast(FP4X4), w1_sc[:, a, P * t : P * (t + 1)]
+
+        th = {}
+        for t in range(PACK):
+            for half in range(HALVES):
+                r1 = product("r1", 2, w1_slice, t, half)
+                th[t, half] = held([P, BANK], F32, "th%d_%d" % (t, half))
+                nc.scalar.activation(th[t, half][:], r1[:], ACT.Tanh)
+
+        w2_bf = [held([P, H * PACK], BF16, "w2_bf%d" % a) for a in range(PASSES)]
+        w2_codes = [held([P, H], U32, "w2_codes%d" % a) for a in range(PASSES)]
+        w2_sc = [held([P, H], U8, "w2_sc%d" % a) for a in range(PASSES)]
+        for raw, (a, c0, c1) in zip(w2_raw, w2_pieces):
+            nc.vector.tensor_copy(
+                w2_bf[a][:].rearrange("p (t m j) -> p m t j", t=PACK, j=PACK)[:, c0 // PACK : c1 // PACK],
+                raw[:].rearrange("p j (m t) -> p m t j", t=PACK),
+            )
+            if c1 == H:
+                for c2, c3 in ((0, H),) if a == 0 else ((0, P), (P, H)):
+                    nc.vector.quantize_mx(
+                        w2_codes[a][:, c2:c3].bitcast(FP8X4), w2_sc[a][:, c2:c3], w2_bf[a][:, PACK * c2 : PACK * c3]
+                    )
+        w3_codes = held([P, PASSES, H], I32, "w3_codes")
+        nc.vector.tensor_copy(
+            w3_codes[:].rearrange("p a (t m) -> p a m t", t=PACK),
+            w3_raw[:].rearrange("p a (m t) -> p a m t", t=PACK),
+        )
+
+        def w2_slice(a, t):
+            return w2_codes[a][:, P * t : P * (t + 1)].bitcast(FP8X4), w2_sc[a][:, P * t : P * (t + 1)]
+
+        def w3_slice(a, t):
+            return w3_codes[:, a, P * t : P * (t + 1)].bitcast(FP8X4), w3_sc[ROWS * a : P, P * t : P * (t + 1)]
+
+        picked1 = held([P, PACK, PAIRS], F32, "picked1")
+        picked2 = held([P, PACK, PAIRS], F32, "picked2")
+        w4_codes = held([P, N], U32, "w4_codes")
+        w4_sc = held([P, N], U8, "w4_sc")
+        for t in range(PACK):
+            h = held([P, S], F32, "h%d" % t)
+            g = gain_sb[:, t : t + 1]
+            for half in range(HALVES):
+                r2 = product("r2", 3, w2_slice, t, half)
+                r3 = product("r3", 3, w3_slice, t, half)
+                sn = ring.tile([P, BANK], F32, name="sn")
+                nc.scalar.activation(sn[:], r2[:], ACT.Sin)
+                u = ring.tile([P, BANK], F32, name="u")
+                nc.vector.scalar_tensor_tensor(u[:], th[t, half][:], g, sn[:], ALU.mult, ALU.mult)
+                nc.vector.scalar_tensor_tensor(
+                    h[:, half * BANK : (half + 1) * BANK], r3[:], g, u[:], ALU.mult, ALU.add
+                )
+            nc.vector.tensor_copy(picked1[:, t, :], h[:].indirect(lists["pos1"][:]))
+            nc.vector.tensor_copy(picked2[:, t, :], h[:].indirect(lists["pos2"][:]))
+            if t in (1, 2):
+                n0 = (t - 1) * (N // 2)
+                w4_bf = held([P, (N // 2) * PACK], BF16, "w4_bf%d" % t)
+                nc.scalar.copy(
+                    w4_bf[:].rearrange("p (c i j) -> p c j i", i=2, j=PACK),
+                    w4_raw[:, :, n0 : n0 + N // 2].rearrange("p j (c i) -> p c j i", i=2),
+                )
+                nc.vector.quantize_mx(
+                    w4_codes[:, n0 : n0 + N // 2].bitcast(FP8X4), w4_sc[:, n0 : n0 + N // 2], w4_bf[:]
+                )
+
+        z_codes = held([P, PAIRS], U32, "z_codes")
+        z_sc = held([P, PAIRS], U8, "z_sc")
+        part = PAIRS // 2
+        z_bf = []
+        for s in range(2):
+            z_bf.append(held([P, part * PACK], BF16, "z_bf%d" % s))
+            cut = slice(s * part, (s + 1) * part)
+            nc.vector.tensor_tensor(
+                z_bf[s][:].rearrange("p (c i t) -> p c t i", i=2, t=PACK),
+                picked1[:, :, cut].rearrange("p t (c i) -> p c t i", i=2),
+                picked2[:, :, cut].rearrange("p t (c i) -> p c t i", i=2),
+                ALU.max,
+            )
+        for s in range(2):
+            cut = slice(s * part, (s + 1) * part)
+            nc.vector.quantize_mx(z_codes[:, cut].bitcast(FP8X4), z_sc[:, cut], z_bf[s][:])
+
+        for n in range(N // P):
+            tag = "r2" if n % 2 == 0 else "r3"
+            acc = psum.tile([P, PAIRS], F32, name=tag, tag=tag, bufs=3)
+            nc.tensor.matmul_mx(
+                acc[:], w4_codes[:, P * n : P * (n + 1)].bitcast(FP8X4), w4_sc[:, P * n : P * (n + 1)],
+                z_codes[:].bitcast(FP8X4), z_sc[:], start=True, stop=True,
+            )
+            y = held([P, PAIRS], F32, "y%d" % n)
+            nc.scalar.copy(y[:], acc[:])
+            rival = held([P, LOTS], F32, "rival%d" % n)
+            nc.vector.tensor_copy(rival[:], y[:].indirect(lists["pos4"][:]))
+            res = held([P, LOTS], F32, "res%d" % n)
+            nc.vector.tensor_tensor(res[:], y[:].indirect(lists["pos3"][:]), rival[:], ALU.subtract)
+            nc.sync.dma_start(out[P * n : P * (n + 1), :], res[:])

@@ -36,8 +36,8 @@ def tile_list_seed_tray_contrast_kernel(
         ring = ctx.enter_context(tc.tile_pool(name="ring", bufs=4))
         psum = ctx.enter_context(tc.psum_pool(name="psum", bufs=1))
 
-        def held(shape, dtype, name):
-            return keep.tile(shape, dtype, name=name, align_bytes=64)
+        def held(shape, dtype, name, tag=""):
+            return keep.tile(shape, dtype, name=name, tag=tag or name, align_bytes=64)
 
         tab_sc = held([P, T], U8, "tab_sc")
         nc.vector.memset(tab_sc[:].bitcast(I32), 0)
@@ -54,9 +54,9 @@ def tile_list_seed_tray_contrast_kernel(
             lists[name] = keep.tile(list(src.shape), U16, name=name)
             nc.sync.dma_start(lists[name][:], src)
 
-        def load_packed_scales(plane, scales):
+        def load_packed_scales(queue, plane, scales):
             for q in range(QUADS):
-                nc.sync.dma_start(
+                queue.dma_start(
                     plane[32 * q : 32 * q + PASSES * ROWS, :].bitcast(I32),
                     scales[:, ROWS * q : ROWS * (q + 1), :].bitcast(I32),
                 )
@@ -66,61 +66,81 @@ def tile_list_seed_tray_contrast_kernel(
             nc.sync.dma_start(words[:], tab_words[a].rearrange("p t i -> p (t i)").bitcast(I32))
             return words
 
+        def load_w2(a):
+            raw = held([P, PACK, H], F32, "w2_raw%d" % a)
+            rows = w2[a * P * PACK : (a + 1) * P * PACK, :]
+            nc.sync.dma_start(raw[:], rows.rearrange("(p j) c -> p j c", j=PACK))
+            return raw
+
+        w2_raw = [load_w2(0)]
         w1_raw = held([P, PASSES, 2 * H], U8, "w1_raw")
         nc.sync.dma_start(w1_raw[:].bitcast(I32), w1_words.rearrange("a p c -> p a c").bitcast(I32))
+        w2_raw.append(load_w2(1))
         load_list("offs", offs)
-        load_list("pos1", pos1)
-        load_packed_scales(tab_sc, tab_scales)
+        load_packed_scales(nc.sync, tab_sc, tab_scales)
         tab = [load_table(0)]
         for q in range(QUADS):
             nc.sync.dma_start(
                 w1_sc_raw[32 * q : 32 * q + ROWS, :, :].bitcast(I32),
                 w1_scales[:, ROWS * q : ROWS * (q + 1), :].rearrange("a r c -> r a c").bitcast(I32),
             )
-        load_list("pos2", pos2)
         tab.append(load_table(1))
-        load_packed_scales(w3_sc_raw, w3_scales)
-        w2_pieces = ((0, 0, H), (1, 0, H // 2), (1, H // 2, H))
-        w2_raw = []
-        for a, c0, c1 in w2_pieces:
-            w2_raw.append(held([P, PACK, c1 - c0], F32, "w2_raw%d_%d" % (a, c0)))
-            rows = w2[a * P * PACK : (a + 1) * P * PACK, c0:c1]
-            nc.sync.dma_start(w2_raw[-1][:], rows.rearrange("(p j) c -> p j c", j=PACK))
-        w3_raw = held([P, PASSES, H], I32, "w3_raw")
-        nc.sync.dma_start(w3_raw[:], w3_words.rearrange("a p c i -> p a (c i)").bitcast(I32))
+        for name, src in (("pos1", pos1), ("pos2", pos2), ("pos3", pos3), ("pos4", pos4)):
+            load_list(name, src)
+        load_packed_scales(nc.gpsimd, w3_sc_raw, w3_scales)
         gain_sb = held([P, PACK], F32, "gain_sb")
-        nc.sync.dma_start(gain_sb[:], gain.rearrange("(p t) -> p t", t=PACK))
-        w4_raw = held([P, PACK, N], F32, "w4_raw")
-        nc.sync.dma_start(w4_raw[:], w4.rearrange("(p j) n -> p j n", j=PACK))
-        load_list("pos3", pos3)
-        load_list("pos4", pos4)
+        nc.gpsimd.dma_start(gain_sb[:], gain.rearrange("(p t) -> p t", t=PACK))
 
-        v_sc0 = held([P, S], U8, "v_sc0")
-        nc.vector.tensor_copy(v_sc0[:], tab_sc[:].indirect(lists["offs"][:]))
-        live = 32 * (QUADS - 1) + ROWS
-        nc.scalar.dma_start(v_sc1[0:live, :].bitcast(I32), v_sc0[ROWS : ROWS + live, :].bitcast(I32))
-        v_sc = (v_sc0, v_sc1)
         w1_codes = held([P, PASSES, 2 * H], U8, "w1_codes")
         nc.vector.tensor_copy(
             w1_codes[:].rearrange("p a (t m b) -> p a t m b", t=PACK, b=2),
             w1_raw[:].rearrange("p a (m t b) -> p a t m b", t=PACK, b=2),
         )
+        warm = held([P, 1], F32, "warm")
+        nc.scalar.activation(warm[:], w2_raw[0][:, 0, 0:1], ACT.Silu)
+        v_sc0 = held([P, S], U8, "v_sc0")
+        nc.vector.tensor_copy(v_sc0[:], tab_sc[:].indirect(lists["offs"][:]))
+        span = 112
+        nc.sync.dma_start(v_sc1[0:span, :].bitcast(I32), v_sc0[ROWS : ROWS + span, :].bitcast(I32))
+        w2_codes, w2_sc = [], []
+        for a in range(PASSES):
+            w2_bf = held([P, H * PACK], BF16, "w2_bf%d" % a)
+            nc.scalar.copy(
+                w2_bf[:].rearrange("p (t m j) -> p m t j", t=PACK, j=PACK),
+                w2_raw[a][:].rearrange("p j (m t) -> p m t j", t=PACK),
+            )
+            w2_codes.append(held([P, H], U32, "w2_codes%d" % a, tag=("w1_raw", "tab_sc")[a]))
+            w2_sc.append(held([P, H], U8, "w2_sc%d" % a))
+            nc.vector.quantize_mx(w2_codes[a][:].bitcast(FP8X4), w2_sc[a][:], w2_bf[:])
+        late = held([P, (PACK * PASSES + PASSES + 1) * H], U8, "late", tag="w2_bf1")
+        w3_raw = late[:, 0 : PACK * PASSES * H].bitcast(I32).rearrange("p (a c) -> p a c", a=PASSES)
+        w1_sc = late[:, PACK * PASSES * H : (PACK + 1) * PASSES * H].rearrange("p (a c) -> p a c", a=PASSES)
+        w3_sc = late[:, (PACK + 1) * PASSES * H :]
+        nc.sync.dma_start(w3_raw, w3_words.rearrange("a p c i -> p a (c i)").bitcast(I32))
+        v_sc = (v_sc0, v_sc1)
         v = {}
         cols = BANK // STRIPE
-        for a in range(PASSES):
-            for half in range(HALVES):
-                v[a, half] = held([P, BANK], U32, "v%d_%d" % (a, half))
-                picks = lists["offs"][:, half * cols : (half + 1) * cols]
-                nc.vector.tensor_copy(v[a, half][:], tab[a][:].bitcast(U32).indirect(picks))
-        w1_sc = held([P, PASSES, H], U8, "w1_sc")
         nc.vector.tensor_copy(
-            w1_sc[:].rearrange("p a (t m) -> p a t m", t=PACK),
+            w1_sc.rearrange("p a (t m) -> p a t m", t=PACK),
             w1_sc_raw[:].rearrange("p a (m t) -> p a t m", t=PACK),
         )
-        w3_sc = held([P, H], U8, "w3_sc")
+        for a, source in enumerate(("w1_sc_raw", "tab0")):
+            words = held([P, S], U32, "v%d" % a, tag=source)
+            for half in range(HALVES):
+                v[a, half] = words[:, half * BANK : (half + 1) * BANK]
+                picks = lists["offs"][:, half * cols : (half + 1) * cols]
+                nc.vector.tensor_copy(v[a, half], tab[a][:].bitcast(U32).indirect(picks))
+            if a == 0:
+                nc.vector.tensor_copy(
+                    w3_sc.rearrange("p (t m) -> p t m", t=PACK),
+                    w3_sc_raw[:].rearrange("p (m t) -> p t m", t=PACK),
+                )
+                w4_raw = held([P, PACK, N], F32, "w4_raw", tag="w3_sc_raw")
+                nc.sync.dma_start(w4_raw[:], w4.rearrange("(p j) n -> p j n", j=PACK))
+        w3_codes = held([P, PASSES, H], I32, "w3_codes", tag="tab1")
         nc.vector.tensor_copy(
-            w3_sc[:].rearrange("p (t m) -> p t m", t=PACK),
-            w3_sc_raw[:].rearrange("p (m t) -> p t m", t=PACK),
+            w3_codes[:].rearrange("p a (t m) -> p a m t", t=PACK),
+            w3_raw.rearrange("p a (m t) -> p a m t", t=PACK),
         )
 
         def product(tag, bufs, weights, t, half):
@@ -129,39 +149,13 @@ def tile_list_seed_tray_contrast_kernel(
                 codes, scales = weights(a, t)
                 nc.tensor.matmul_mx(
                     acc[:], codes, scales,
-                    v[a, half][:].bitcast(FP8X4), v_sc[a][:, half * BANK : (half + 1) * BANK],
+                    v[a, half].bitcast(FP8X4), v_sc[a][:, half * BANK : (half + 1) * BANK],
                     start=(a == 0), stop=(a == PASSES - 1),
                 )
             return acc
 
         def w1_slice(a, t):
             return w1_codes[:, a, 2 * P * t : 2 * P * (t + 1)].bitcast(FP4X4), w1_sc[:, a, P * t : P * (t + 1)]
-
-        th = {}
-        for t in range(PACK):
-            for half in range(HALVES):
-                r1 = product("r1", 2, w1_slice, t, half)
-                th[t, half] = held([P, BANK], F32, "th%d_%d" % (t, half))
-                nc.scalar.activation(th[t, half][:], r1[:], ACT.Tanh)
-
-        w2_bf = [held([P, H * PACK], BF16, "w2_bf%d" % a) for a in range(PASSES)]
-        w2_codes = [held([P, H], U32, "w2_codes%d" % a) for a in range(PASSES)]
-        w2_sc = [held([P, H], U8, "w2_sc%d" % a) for a in range(PASSES)]
-        for raw, (a, c0, c1) in zip(w2_raw, w2_pieces):
-            nc.vector.tensor_copy(
-                w2_bf[a][:].rearrange("p (t m j) -> p m t j", t=PACK, j=PACK)[:, c0 // PACK : c1 // PACK],
-                raw[:].rearrange("p j (m t) -> p m t j", t=PACK),
-            )
-            if c1 == H:
-                for c2, c3 in ((0, H),) if a == 0 else ((0, P), (P, H)):
-                    nc.vector.quantize_mx(
-                        w2_codes[a][:, c2:c3].bitcast(FP8X4), w2_sc[a][:, c2:c3], w2_bf[a][:, PACK * c2 : PACK * c3]
-                    )
-        w3_codes = held([P, PASSES, H], I32, "w3_codes")
-        nc.vector.tensor_copy(
-            w3_codes[:].rearrange("p a (t m) -> p a m t", t=PACK),
-            w3_raw[:].rearrange("p a (m t) -> p a m t", t=PACK),
-        )
 
         def w2_slice(a, t):
             return w2_codes[a][:, P * t : P * (t + 1)].bitcast(FP8X4), w2_sc[a][:, P * t : P * (t + 1)]
@@ -177,19 +171,27 @@ def tile_list_seed_tray_contrast_kernel(
             h = held([P, S], F32, "h%d" % t)
             g = gain_sb[:, t : t + 1]
             for half in range(HALVES):
-                r2 = product("r2", 3, w2_slice, t, half)
-                r3 = product("r3", 3, w3_slice, t, half)
+                r1 = product("r1", 2, w1_slice, t, half)
+                r2 = product("r2", 2, w2_slice, t, half)
+                r3 = product("r3", 4, w3_slice, t, half)
+                th = ring.tile([P, BANK], F32, name="th")
+                nc.scalar.activation(th[:], r1[:], ACT.Tanh)
                 sn = ring.tile([P, BANK], F32, name="sn")
                 nc.scalar.activation(sn[:], r2[:], ACT.Sin)
                 u = ring.tile([P, BANK], F32, name="u")
-                nc.vector.scalar_tensor_tensor(u[:], th[t, half][:], g, sn[:], ALU.mult, ALU.mult)
+                if t == 0:
+                    nc.vector.scalar_tensor_tensor(u[:], th[:], g, sn[:], ALU.mult, ALU.mult)
+                else:
+                    tg = ring.tile([P, BANK], F32, name="tg")
+                    nc.gpsimd.tensor_scalar(tg[:], th[:], g, 0.0, ALU.mult, ALU.add)
+                    nc.gpsimd.tensor_tensor(u[:], tg[:], sn[:], ALU.mult)
                 nc.vector.scalar_tensor_tensor(
                     h[:, half * BANK : (half + 1) * BANK], r3[:], g, u[:], ALU.mult, ALU.add
                 )
             nc.vector.tensor_copy(picked1[:, t, :], h[:].indirect(lists["pos1"][:]))
             nc.vector.tensor_copy(picked2[:, t, :], h[:].indirect(lists["pos2"][:]))
-            if t in (1, 2):
-                n0 = (t - 1) * (N // 2)
+            if t >= 2:
+                n0 = (t - 2) * (N // 2)
                 w4_bf = held([P, (N // 2) * PACK], BF16, "w4_bf%d" % t)
                 nc.scalar.copy(
                     w4_bf[:].rearrange("p (c i j) -> p c j i", i=2, j=PACK),
@@ -217,8 +219,7 @@ def tile_list_seed_tray_contrast_kernel(
             nc.vector.quantize_mx(z_codes[:, cut].bitcast(FP8X4), z_sc[:, cut], z_bf[s][:])
 
         for n in range(N // P):
-            tag = "r2" if n % 2 == 0 else "r3"
-            acc = psum.tile([P, PAIRS], F32, name=tag, tag=tag, bufs=3)
+            acc = psum.tile([P, PAIRS], F32, name="acc", tag="r3", bufs=4)
             nc.tensor.matmul_mx(
                 acc[:], w4_codes[:, P * n : P * (n + 1)].bitcast(FP8X4), w4_sc[:, P * n : P * (n + 1)],
                 z_codes[:].bitcast(FP8X4), z_sc[:], start=True, stop=True,
@@ -228,5 +229,10 @@ def tile_list_seed_tray_contrast_kernel(
             rival = held([P, LOTS], F32, "rival%d" % n)
             nc.vector.tensor_copy(rival[:], y[:].indirect(lists["pos4"][:]))
             res = held([P, LOTS], F32, "res%d" % n)
-            nc.vector.tensor_tensor(res[:], y[:].indirect(lists["pos3"][:]), rival[:], ALU.subtract)
+            if n < N // P - 1:
+                lot = held([P, LOTS], F32, "lot%d" % n)
+                nc.vector.tensor_copy(lot[:], y[:].indirect(lists["pos3"][:]))
+                nc.gpsimd.tensor_tensor(res[:], lot[:], rival[:], ALU.subtract)
+            else:
+                nc.vector.tensor_tensor(res[:], y[:].indirect(lists["pos3"][:]), rival[:], ALU.subtract)
             nc.sync.dma_start(out[P * n : P * (n + 1), :], res[:])

@@ -183,56 +183,60 @@ def tile_list_seed_tray_contrast_kernel(
                     nc.vector.scalar_tensor_tensor(u[:], th[:], g, sn[:], ALU.mult, ALU.mult)
                 else:
                     tg = ring.tile([P, BANK], F32, name="tg")
-                    nc.gpsimd.tensor_scalar(tg[:], th[:], g, 0.0, ALU.mult, ALU.add)
+                    nc.scalar.activation(tg[:], th[:], ACT.Copy, scale=g)
                     nc.gpsimd.tensor_tensor(u[:], tg[:], sn[:], ALU.mult)
                 nc.vector.scalar_tensor_tensor(
                     h[:, half * BANK : (half + 1) * BANK], r3[:], g, u[:], ALU.mult, ALU.add
                 )
             nc.vector.tensor_copy(picked1[:, t, :], h[:].indirect(lists["pos1"][:]))
             nc.vector.tensor_copy(picked2[:, t, :], h[:].indirect(lists["pos2"][:]))
-            if t >= 2:
-                n0 = (t - 2) * (N // 2)
-                w4_bf = held([P, (N // 2) * PACK], BF16, "w4_bf%d" % t)
-                nc.scalar.copy(
-                    w4_bf[:].rearrange("p (c i j) -> p c j i", i=2, j=PACK),
-                    w4_raw[:, :, n0 : n0 + N // 2].rearrange("p j (c i) -> p c j i", i=2),
-                )
-                nc.vector.quantize_mx(
-                    w4_codes[:, n0 : n0 + N // 2].bitcast(FP8X4), w4_sc[:, n0 : n0 + N // 2], w4_bf[:]
-                )
 
         z_codes = held([P, PAIRS], U32, "z_codes")
         z_sc = held([P, PAIRS], U8, "z_sc")
-        part = PAIRS // 2
-        z_bf = []
-        for s in range(2):
-            z_bf.append(held([P, part * PACK], BF16, "z_bf%d" % s))
-            cut = slice(s * part, (s + 1) * part)
+        tiles = N // P
+        banks = [("r3", 4)] * 4 + [("r1", 2), ("r2", 2)]
+        acc = [psum.tile([P, PAIRS], F32, name="y_acc%d" % n, tag=banks[n][0], bufs=banks[n][1]) for n in range(tiles)]
+        y = [held([P, PAIRS], F32, "y%d" % n) for n in range(tiles)]
+
+        def second_stage(n, cut):
+            nc.tensor.matmul_mx(
+                acc[n][:, cut], w4_codes[:, P * n : P * (n + 1)].bitcast(FP8X4), w4_sc[:, P * n : P * (n + 1)],
+                z_codes[:, cut].bitcast(FP8X4), z_sc[:, cut], start=True, stop=True,
+            )
+            nc.scalar.copy(y[n][:, cut], acc[n][:, cut])
+
+        cuts = [slice(s * PAIRS // 2, (s + 1) * PAIRS // 2) for s in range(2)]
+        for s, cut in enumerate(cuts):
+            z_bf = held([P, PAIRS // 2 * PACK], BF16, "z_bf%d" % s)
             nc.vector.tensor_tensor(
-                z_bf[s][:].rearrange("p (c i t) -> p c t i", i=2, t=PACK),
+                z_bf[:].rearrange("p (c i t) -> p c t i", i=2, t=PACK),
                 picked1[:, :, cut].rearrange("p t (c i) -> p c t i", i=2),
                 picked2[:, :, cut].rearrange("p t (c i) -> p c t i", i=2),
                 ALU.max,
             )
-        for s in range(2):
-            cut = slice(s * part, (s + 1) * part)
-            nc.vector.quantize_mx(z_codes[:, cut].bitcast(FP8X4), z_sc[:, cut], z_bf[s][:])
-
-        for n in range(N // P):
-            acc = psum.tile([P, PAIRS], F32, name="acc", tag="r3", bufs=4)
-            nc.tensor.matmul_mx(
-                acc[:], w4_codes[:, P * n : P * (n + 1)].bitcast(FP8X4), w4_sc[:, P * n : P * (n + 1)],
-                z_codes[:].bitcast(FP8X4), z_sc[:], start=True, stop=True,
+            outs = slice(s * N // 2, (s + 1) * N // 2)
+            w4_bf = held([P, N // 2 * PACK], BF16, "w4_bf%d" % s)
+            nc.scalar.copy(
+                w4_bf[:].rearrange("p (c i j) -> p c j i", i=2, j=PACK),
+                w4_raw[:, :, outs].rearrange("p j (c i) -> p c j i", i=2),
             )
-            y = held([P, PAIRS], F32, "y%d" % n)
-            nc.scalar.copy(y[:], acc[:])
+            nc.vector.quantize_mx(w4_codes[:, outs].bitcast(FP8X4), w4_sc[:, outs], w4_bf[:])
+            nc.vector.quantize_mx(z_codes[:, cut].bitcast(FP8X4), z_sc[:, cut], z_bf[:])
+            if s == 0:
+                for n in range(tiles // 2):
+                    second_stage(n, cuts[0])
+
+        for n in range(tiles):
+            if n >= tiles // 2:
+                second_stage(n, cuts[0])
+            second_stage(n, cuts[1])
             rival = held([P, LOTS], F32, "rival%d" % n)
-            nc.vector.tensor_copy(rival[:], y[:].indirect(lists["pos4"][:]))
+            nc.vector.tensor_copy(rival[:], y[n][:].indirect(lists["pos4"][:]))
             res = held([P, LOTS], F32, "res%d" % n)
-            if n < N // P - 1:
+            if n < tiles - 1:
                 lot = held([P, LOTS], F32, "lot%d" % n)
-                nc.vector.tensor_copy(lot[:], y[:].indirect(lists["pos3"][:]))
+                nc.vector.tensor_copy(lot[:], y[n][:].indirect(lists["pos3"][:]))
                 nc.gpsimd.tensor_tensor(res[:], lot[:], rival[:], ALU.subtract)
             else:
-                nc.vector.tensor_tensor(res[:], y[:].indirect(lists["pos3"][:]), rival[:], ALU.subtract)
+                nc.vector.tensor_tensor(res[:], y[n][:].indirect(lists["pos3"][:]), rival[:], ALU.subtract)
             nc.sync.dma_start(out[P * n : P * (n + 1), :], res[:])

@@ -165,8 +165,6 @@ def tile_list_seed_tray_contrast_kernel(
 
         picked1 = held([P, PACK, PAIRS], F32, "picked1")
         picked2 = held([P, PACK, PAIRS], F32, "picked2")
-        w4_codes = held([P, N], U32, "w4_codes")
-        w4_sc = held([P, N], U8, "w4_sc")
         for t in range(PACK):
             h = held([P, S], F32, "h%d" % t)
             g = gain_sb[:, t : t + 1]
@@ -191,52 +189,45 @@ def tile_list_seed_tray_contrast_kernel(
             nc.vector.tensor_copy(picked1[:, t, :], h[:].indirect(lists["pos1"][:]))
             nc.vector.tensor_copy(picked2[:, t, :], h[:].indirect(lists["pos2"][:]))
 
+        w4_bf = held([P, N * PACK], BF16, "w4_bf")
+        third = N // 3
+        for n0 in range(0, N, third):
+            nc.scalar.copy(
+                w4_bf[:, PACK * n0 : PACK * (n0 + third)].rearrange("p (c i j) -> p c j i", i=2, j=PACK),
+                w4_raw[:, :, n0 : n0 + third].rearrange("p j (c i) -> p c j i", i=2),
+            )
+
+        def quantize_w4(n0, n1, after):
+            codes = held([P, n1 - n0], U32, "w4_codes%d" % n0, tag=after)
+            scales = held([P, n1 - n0], U8, "w4_sc%d" % n0)
+            nc.vector.quantize_mx(codes[:].bitcast(FP8X4), scales[:], w4_bf[:, PACK * n0 : PACK * n1])
+            return [(codes[:, c : c + P].bitcast(FP8X4), scales[:, c : c + P]) for c in range(0, n1 - n0, P)]
+
+        z_bf = held([P, PAIRS * PACK], BF16, "z_bf")
+        nc.vector.tensor_tensor(
+            z_bf[:].rearrange("p (c i t) -> p c t i", i=2, t=PACK),
+            picked1[:].rearrange("p t (c i) -> p c t i", i=2),
+            picked2[:].rearrange("p t (c i) -> p c t i", i=2),
+            ALU.max,
+        )
+        w4_tiles = quantize_w4(0, third, "h%d" % (PACK - 1))
         z_codes = held([P, PAIRS], U32, "z_codes")
         z_sc = held([P, PAIRS], U8, "z_sc")
-        tiles = N // P
-        banks = [("r3", 4)] * 4 + [("r1", 2), ("r2", 2)]
-        acc = [psum.tile([P, PAIRS], F32, name="y_acc%d" % n, tag=banks[n][0], bufs=banks[n][1]) for n in range(tiles)]
-        y = [held([P, PAIRS], F32, "y%d" % n) for n in range(tiles)]
+        nc.vector.quantize_mx(z_codes[:].bitcast(FP8X4), z_sc[:], z_bf[:])
+        w4_tiles = w4_tiles + quantize_w4(third, N, "z_bf")
 
-        def second_stage(n, cut):
-            nc.tensor.matmul_mx(
-                acc[n][:, cut], w4_codes[:, P * n : P * (n + 1)].bitcast(FP8X4), w4_sc[:, P * n : P * (n + 1)],
-                z_codes[:, cut].bitcast(FP8X4), z_sc[:, cut], start=True, stop=True,
-            )
-            nc.scalar.copy(y[n][:, cut], acc[n][:, cut])
-
-        cuts = [slice(s * PAIRS // 2, (s + 1) * PAIRS // 2) for s in range(2)]
-        for s, cut in enumerate(cuts):
-            z_bf = held([P, PAIRS // 2 * PACK], BF16, "z_bf%d" % s)
-            nc.vector.tensor_tensor(
-                z_bf[:].rearrange("p (c i t) -> p c t i", i=2, t=PACK),
-                picked1[:, :, cut].rearrange("p t (c i) -> p c t i", i=2),
-                picked2[:, :, cut].rearrange("p t (c i) -> p c t i", i=2),
-                ALU.max,
-            )
-            outs = slice(s * N // 2, (s + 1) * N // 2)
-            w4_bf = held([P, N // 2 * PACK], BF16, "w4_bf%d" % s)
-            nc.scalar.copy(
-                w4_bf[:].rearrange("p (c i j) -> p c j i", i=2, j=PACK),
-                w4_raw[:, :, outs].rearrange("p j (c i) -> p c j i", i=2),
-            )
-            nc.vector.quantize_mx(w4_codes[:, outs].bitcast(FP8X4), w4_sc[:, outs], w4_bf[:])
-            nc.vector.quantize_mx(z_codes[:, cut].bitcast(FP8X4), z_sc[:, cut], z_bf[:])
-            if s == 0:
-                for n in range(tiles // 2):
-                    second_stage(n, cuts[0])
-
-        for n in range(tiles):
-            if n >= tiles // 2:
-                second_stage(n, cuts[0])
-            second_stage(n, cuts[1])
+        for n, (codes, scales) in enumerate(w4_tiles):
+            acc = psum.tile([P, PAIRS], F32, name="acc", tag="r3", bufs=4)
+            nc.tensor.matmul_mx(acc[:], codes, scales, z_codes[:].bitcast(FP8X4), z_sc[:], start=True, stop=True)
+            y = held([P, PAIRS], F32, "y%d" % n)
+            nc.scalar.copy(y[:], acc[:])
             rival = held([P, LOTS], F32, "rival%d" % n)
-            nc.vector.tensor_copy(rival[:], y[n][:].indirect(lists["pos4"][:]))
+            nc.vector.tensor_copy(rival[:], y[:].indirect(lists["pos4"][:]))
             res = held([P, LOTS], F32, "res%d" % n)
-            if n < tiles - 1:
+            if n < len(w4_tiles) - 1:
                 lot = held([P, LOTS], F32, "lot%d" % n)
-                nc.vector.tensor_copy(lot[:], y[n][:].indirect(lists["pos3"][:]))
+                nc.vector.tensor_copy(lot[:], y[:].indirect(lists["pos3"][:]))
                 nc.gpsimd.tensor_tensor(res[:], lot[:], rival[:], ALU.subtract)
             else:
-                nc.vector.tensor_tensor(res[:], y[n][:].indirect(lists["pos3"][:]), rival[:], ALU.subtract)
+                nc.vector.tensor_tensor(res[:], y[:].indirect(lists["pos3"][:]), rival[:], ALU.subtract)
             nc.sync.dma_start(out[P * n : P * (n + 1), :], res[:])

from contextlib import ExitStack

import concourse.mybir as mybir

K, T, S, H, PAIRS, N, LOTS = 1024, 4096, 1024, 512, 512, 768, 256
FLOPS = 2 * (3 * K * H * S + H * N * PAIRS)

F32 = mybir.dt.float32
BF16 = mybir.dt.bfloat16
I32 = mybir.dt.int32
U32 = mybir.dt.uint32
U16 = mybir.dt.uint16
U8 = mybir.dt.uint8
FP8X4 = mybir.dt.float8_e4m3fn_x4
FP4X4 = mybir.dt.float4_e2m1fn_x4
ACT = mybir.ActivationFunctionType
ALU = mybir.AluOpType

P = 128
PACK = 4
PASSES = K // (P * PACK)
BANK = 512
HALVES = S // BANK
QUADS = 4
ROWS = 4
STRIPE = 16


def tile_list_seed_tray_contrast_kernel(
    tc, tab_words, tab_scales, offs, pos1, pos2, pos3, pos4,
    w1_words, w1_scales, w2, w3_words, w3_scales, gain, w4, out,
):
    nc = tc.nc
    with ExitStack() as ctx:
        keep = ctx.enter_context(tc.tile_pool(name="keep", bufs=1))
        ring = ctx.enter_context(tc.tile_pool(name="ring", bufs=4))
        psum = ctx.enter_context(tc.psum_pool(name="psum", bufs=1))

        def held(shape, dtype, name, tag=""):
            return keep.tile(shape, dtype, name=name, tag=tag or name, align_bytes=64)

        tab_sc = held([P, T], U8, "tab_sc")
        nc.vector.memset(tab_sc[:].bitcast(I32), 0)
        w1_sc_raw = held([P, PASSES, H], U8, "w1_sc_raw")
        nc.gpsimd.memset(w1_sc_raw[:].bitcast(I32), 0)
        w3_sc_raw = held([P, H], U8, "w3_sc_raw")
        nc.gpsimd.memset(w3_sc_raw[:].bitcast(I32), 0)
        v_sc1 = held([P, S], U8, "v_sc1")
        nc.gpsimd.memset(v_sc1[:].bitcast(I32), 0)

        lists = {}

        def load_list(name, src):
            lists[name] = keep.tile(list(src.shape), U16, name=name)
            nc.sync.dma_start(lists[name][:], src)

        def load_packed_scales(queue, plane, scales):
            for q in range(QUADS):
                queue.dma_start(
                    plane[32 * q : 32 * q + PASSES * ROWS, :].bitcast(I32),
                    scales[:, ROWS * q : ROWS * (q + 1), :].bitcast(I32),
                )

        def load_table(a):
            words = held([P, T], I32, "tab%d" % a)
            nc.sync.dma_start(words[:], tab_words[a].rearrange("p t i -> p (t i)").bitcast(I32))
            return words

        def load_w2(a):
            raw = held([P, PACK, H], F32, "w2_raw%d" % a)
            rows = w2[a * P * PACK : (a + 1) * P * PACK, :]
            nc.sync.dma_start(raw[:], rows.rearrange("(p j) c -> p j c", j=PACK))
            return raw

        w2_raw = [load_w2(0)]
        w1_raw = held([P, PASSES, 2 * H], U8, "w1_raw")
        nc.sync.dma_start(w1_raw[:].bitcast(I32), w1_words.rearrange("a p c -> p a c").bitcast(I32))
        w2_raw.append(load_w2(1))
        load_list("offs", offs)
        load_packed_scales(nc.sync, tab_sc, tab_scales)
        tab = [load_table(0)]
        for q in range(QUADS):
            nc.sync.dma_start(
                w1_sc_raw[32 * q : 32 * q + ROWS, :, :].bitcast(I32),
                w1_scales[:, ROWS * q : ROWS * (q + 1), :].rearrange("a r c -> r a c").bitcast(I32),
            )
        tab.append(load_table(1))
        for name, src in (("pos1", pos1), ("pos2", pos2), ("pos3", pos3), ("pos4", pos4)):
            load_list(name, src)
        load_packed_scales(nc.gpsimd, w3_sc_raw, w3_scales)
        gain_sb = held([P, PACK], F32, "gain_sb")
        nc.gpsimd.dma_start(gain_sb[:], gain.rearrange("(p t) -> p t", t=PACK))

        w1_codes = held([P, PASSES, 2 * H], U8, "w1_codes")
        nc.vector.tensor_copy(
            w1_codes[:].rearrange("p a (t m b) -> p a t m b", t=PACK, b=2),
            w1_raw[:].rearrange("p a (m t b) -> p a t m b", t=PACK, b=2),
        )
        warm = held([P, 1], F32, "warm")
        nc.scalar.activation(warm[:], w2_raw[0][:, 0, 0:1], ACT.Silu)
        v_sc0 = held([P, S], U8, "v_sc0")
        nc.vector.tensor_copy(v_sc0[:], tab_sc[:].indirect(lists["offs"][:]))
        span = 112
        nc.sync.dma_start(v_sc1[0:span, :].bitcast(I32), v_sc0[ROWS : ROWS + span, :].bitcast(I32))
        w2_codes, w2_sc = [], []
        for a in range(PASSES):
            w2_bf = held([P, H * PACK], BF16, "w2_bf%d" % a)
            nc.scalar.copy(
                w2_bf[:].rearrange("p (t m j) -> p m t j", t=PACK, j=PACK),
                w2_raw[a][:].rearrange("p j (m t) -> p m t j", t=PACK),
            )
            w2_codes.append(held([P, H], U32, "w2_codes%d" % a, tag=("w1_raw", "tab_sc")[a]))
            w2_sc.append(held([P, H], U8, "w2_sc%d" % a))
            nc.vector.quantize_mx(w2_codes[a][:].bitcast(FP8X4), w2_sc[a][:], w2_bf[:])
        late = held([P, (PACK * PASSES + PASSES + 1) * H], U8, "late", tag="w2_bf1")
        w3_raw = late[:, 0 : PACK * PASSES * H].bitcast(I32).rearrange("p (a c) -> p a c", a=PASSES)
        w1_sc = late[:, PACK * PASSES * H : (PACK + 1) * PASSES * H].rearrange("p (a c) -> p a c", a=PASSES)
        w3_sc = late[:, (PACK + 1) * PASSES * H :]
        nc.sync.dma_start(w3_raw, w3_words.rearrange("a p c i -> p a (c i)").bitcast(I32))
        v_sc = (v_sc0, v_sc1)
        v = {}
        cols = BANK // STRIPE
        nc.vector.tensor_copy(
            w1_sc.rearrange("p a (t m) -> p a t m", t=PACK),
            w1_sc_raw[:].rearrange("p a (m t) -> p a t m", t=PACK),
        )
        for a, source in enumerate(("w1_sc_raw", "tab0")):
            words = held([P, S], U32, "v%d" % a, tag=source)
            for half in range(HALVES):
                v[a, half] = words[:, half * BANK : (half + 1) * BANK]
                picks = lists["offs"][:, half * cols : (half + 1) * cols]
                nc.vector.tensor_copy(v[a, half], tab[a][:].bitcast(U32).indirect(picks))
            if a == 0:
                nc.vector.tensor_copy(
                    w3_sc.rearrange("p (t m) -> p t m", t=PACK),
                    w3_sc_raw[:].rearrange("p (m t) -> p t m", t=PACK),
                )
                w4_raw = held([P, PACK, N], F32, "w4_raw", tag="w3_sc_raw")
                nc.sync.dma_start(w4_raw[:], w4.rearrange("(p j) n -> p j n", j=PACK))
        w3_codes = held([P, PASSES, H], I32, "w3_codes", tag="tab1")
        nc.vector.tensor_copy(
            w3_codes[:].rearrange("p a (t m) -> p a m t", t=PACK),
            w3_raw.rearrange("p a (m t) -> p a m t", t=PACK),
        )

        def product(tag, bufs, weights, t, half):
            acc = psum.tile([P, BANK], F32, name=tag, tag=tag, bufs=bufs)
            for a in range(PASSES):
                codes, scales = weights(a, t)
                nc.tensor.matmul_mx(
                    acc[:], codes, scales,
                    v[a, half].bitcast(FP8X4), v_sc[a][:, half * BANK : (half + 1) * BANK],
                    start=(a == 0), stop=(a == PASSES - 1),
                )
            return acc

        def w1_slice(a, t):
            return w1_codes[:, a, 2 * P * t : 2 * P * (t + 1)].bitcast(FP4X4), w1_sc[:, a, P * t : P * (t + 1)]

        def w2_slice(a, t):
            return w2_codes[a][:, P * t : P * (t + 1)].bitcast(FP8X4), w2_sc[a][:, P * t : P * (t + 1)]

        def w3_slice(a, t):
            return w3_codes[:, a, P * t : P * (t + 1)].bitcast(FP8X4), w3_sc[ROWS * a : P, P * t : P * (t + 1)]

        picked1 = held([P, PACK, PAIRS], F32, "picked1")
        picked2 = held([P, PACK, PAIRS], F32, "picked2")
        for t in range(PACK):
            h = held([P, S], F32, "h%d" % t)
            g = gain_sb[:, t : t + 1]
            for half in range(HALVES):
                r1 = product("r1", 2, w1_slice, t, half)
                r2 = product("r2", 2, w2_slice, t, half)
                r3 = product("r3", 4, w3_slice, t, half)
                th = ring.tile([P, BANK], F32, name="th")
                nc.scalar.activation(th[:], r1[:], ACT.Tanh)
                sn = ring.tile([P, BANK], F32, name="sn")
                nc.scalar.activation(sn[:], r2[:], ACT.Sin)
                u = ring.tile([P, BANK], F32, name="u")
                if t == 0:
                    nc.vector.scalar_tensor_tensor(u[:], th[:], g, sn[:], ALU.mult, ALU.mult)
                else:
                    tg = ring.tile([P, BANK], F32, name="tg")
                    nc.scalar.activation(tg[:], th[:], ACT.Copy, scale=g)
                    nc.gpsimd.tensor_tensor(u[:], tg[:], sn[:], ALU.mult)
                nc.vector.scalar_tensor_tensor(
                    h[:, half * BANK : (half + 1) * BANK], r3[:], g, u[:], ALU.mult, ALU.add
                )
            nc.vector.tensor_copy(picked1[:, t, :], h[:].indirect(lists["pos1"][:]))
            nc.vector.tensor_copy(picked2[:, t, :], h[:].indirect(lists["pos2"][:]))

        w4_bf = held([P, N * PACK], BF16, "w4_bf")
        third = N // 3
        for n0 in range(0, N, third):
            nc.scalar.copy(
                w4_bf[:, PACK * n0 : PACK * (n0 + third)].rearrange("p (c i j) -> p c j i", i=2, j=PACK),
                w4_raw[:, :, n0 : n0 + third].rearrange("p j (c i) -> p c j i", i=2),
            )

        def quantize_w4(n0, n1, after):
            codes = held([P, n1 - n0], U32, "w4_codes%d" % n0, tag=after)
            scales = held([P, n1 - n0], U8, "w4_sc%d" % n0)
            nc.vector.quantize_mx(codes[:].bitcast(FP8X4), scales[:], w4_bf[:, PACK * n0 : PACK * n1])
            return [(codes[:, c : c + P].bitcast(FP8X4), scales[:, c : c + P]) for c in range(0, n1 - n0, P)]

        z_bf = held([P, PAIRS * PACK], BF16, "z_bf")
        nc.vector.tensor_tensor(
            z_bf[:].rearrange("p (c i t) -> p c t i", i=2, t=PACK),
            picked1[:].rearrange("p t (c i) -> p c t i", i=2),
            picked2[:].rearrange("p t (c i) -> p c t i", i=2),
            ALU.max,
        )
        w4_tiles = quantize_w4(0, third, "h%d" % (PACK - 1))
        z_codes = held([P, PAIRS], U32, "z_codes")
        z_sc = held([P, PAIRS], U8, "z_sc")
        nc.vector.quantize_mx(z_codes[:].bitcast(FP8X4), z_sc[:], z_bf[:])
        w4_tiles = w4_tiles + quantize_w4(third, N, "z_bf")

        for n, (codes, scales) in enumerate(w4_tiles):
            acc = psum.tile([P, PAIRS], F32, name="acc", tag="r3", bufs=4)
            nc.tensor.matmul_mx(acc[:], codes, scales, z_codes[:].bitcast(FP8X4), z_sc[:], start=True, stop=True)
            y = held([P, PAIRS], F32, "y%d" % n)
            nc.scalar.copy(y[:], acc[:])
            rival = held([P, LOTS], F32, "rival%d" % n)
            nc.vector.tensor_copy(rival[:], y[:].indirect(lists["pos4"][:]))
            res = held([P, LOTS], F32, "res%d" % n)
            if n < len(w4_tiles) - 1:
                lot = held([P, LOTS], F32, "lot%d" % n)
                nc.vector.tensor_copy(lot[:], y[:].indirect(lists["pos3"][:]))
                nc.gpsimd.tensor_tensor(res[:], lot[:], rival[:], ALU.subtract)
            else:
                nc.vector.tensor_tensor(res[:], y[:].indirect(lists["pos3"][:]), rival[:], ALU.subtract)
            nc.sync.dma_start(out[P * n : P * (n + 1), :], res[:])
